import numpy as np, ml_dtypes
CORES = [2,10,18,26,34,42,50,58]
N = 8
def setup_inputs(rng):
    return {"x1": rng.standard_normal((N, 128, 2), dtype=np.float32), "x2": rng.standard_normal((N, 128, 512), dtype=np.float32).astype(ml_dtypes.bfloat16)}
def reference(x1, x2):
    out = []
    s = x1.sum(axis=0, dtype=np.float64).astype(x1.dtype)
    out.append(np.broadcast_to(s, (N,) + s.shape))
    g = np.concatenate(list(x2), axis=1)
    out.append(np.broadcast_to(g, (N,) + g.shape))
    return {"y1": out[0], "y2": out[1]}

@@ -1,0 +1,111 @@
+import concourse.bass as bass
+
+RANK_K = 2
+FOLD_K = 1
+W = 512
+
+SCRATCH = {
+    "land": ("sbuf", [128, 4096], "bfloat16"),
+    "s1": ("dram", [128, 2], "float32"),
+    "g1": ("dram", [8, 128, 2], "float32"),
+    "r1": ("dram", [128, 2], "float32"),
+}
+SEMAPHORES = ["ld1", "ld2", "st", "snd", "hx", "a01", "a23", "a45", "a67", "g", "r"]
+
+CALLS = {
+    2: [
+        [(0xFF00, ["h6"], "hx"), (0x000F, [2], "a23"), (0x00F0, [1], "a01")],
+        [(0x000F, [4], "a45"), (0x00F0, [3], "a23")],
+        [(0x00FF, [6], "a67")],
+    ],
+    6: [
+        [(0x000F, [5], "a45"), (0x00F0, [7], "a67")],
+    ],
+}
+STORES = [("a01", 0, 2), ("a23", 2, 2), "y1", ("a45", 4, 2), ("a67", 6, 2)]
+
+
+def bits(mask):
+    return bin(mask).count("1")
+
+
+def arrivals(sem):
+    n = 0
+    for calls in CALLS.values():
+        for call in calls:
+            for mask, dsts, s in call:
+                if s == sem:
+                    n += bits(mask) * len(dsts)
+    return n
+
+
+def rank_program(g, core, T, topo):
+    chip, k = topo.chip(core), core % 8
+    r = T.rank_of(8 * chip + RANK_K)
+    if r is None:
+        return
+
+    def did(c):
+        a = topo.addr(c)
+        return bass.DstId(rid=a[0], pnc=a[1])
+
+    def sem(name):
+        return {"hx": T.sem.hx, "a01": T.sem.a01, "a23": T.sem.a23, "a45": T.sem.a45, "a67": T.sem.a67}[name]
+
+    own = T.land[:, W * r:W * (r + 1)]
+    sent = 0
+
+    def send_block():
+        n = 0
+        for call in CALLS[k]:
+            trs = []
+            for mask, dsts, s in call:
+                ids = []
+                for d in dsts:
+                    if isinstance(d, str):
+                        ids.append(did(8 * chip + int(d[1:])))
+                    else:
+                        ids.append(did(T.cores[r ^ d]))
+                trs.append(bass.RemoteDMATransfer(dst_ids=ids, dma_engine_mask=mask, remote_sem=sem(s),
+                                                  srcs=[own], dsts=[own] * len(ids), alu_op=0))
+                n += bits(mask)
+            g.remote_dma_fused(trs, local_sem=T.sem.snd)
+        return n
+
+    if k == FOLD_K:
+        g.wait_ge(T.sem.g, 8)
+        g.remote_dma_fused([bass.RemoteDMATransfer(dst_ids=[did(8 * chip + RANK_K)], dma_engine_mask=1,
+                                                   remote_sem=T.sem.r, srcs=[T.g1[j] for j in range(8)],
+                                                   dsts=[T.r1[:]], alu_op=1)], local_sem=T.sem.snd)
+        g.wait_ge(T.sem.snd, 1)
+        return
+
+    if k != RANK_K:
+        if k in CALLS:
+            g.wait_ge(T.sem.hx, arrivals("hx"))
+            sent = send_block()
+            g.wait_ge(T.sem.snd, sent)
+        return
+
+    g.dma_start(T.s1[:], T.x1[:]).then_inc(T.sem.ld1, 16)
+    g.dma_start(own, T.x2[:]).then_inc(T.sem.ld2, 16)
+    g.wait_ge(T.sem.ld1, 16)
+    g.remote_dma_fused([bass.RemoteDMATransfer(dst_ids=[did(T.cores[j] - RANK_K + FOLD_K)], dma_engine_mask=1 << j,
+                                               remote_sem=T.sem.g, srcs=[T.s1[:]], dsts=[T.g1[r]], alu_op=0)
+                        for j in range(8)], local_sem=T.sem.snd)
+    sent += 8
+    g.wait_ge(T.sem.ld2, 16)
+    sent += send_block()
+    stores = 0
+    for s in STORES:
+        if s == "y1":
+            g.wait_ge(T.sem.r, 1)
+            g.dma_start(T.y1[:], T.r1[:]).then_inc(T.sem.st, 16)
+        else:
+            name, d0, n = s
+            g.wait_ge(sem(name), arrivals(name))
+            c0 = ((r ^ d0) // n) * n * W
+            g.dma_start(T.y2[:, c0:c0 + n * W], T.land[:, c0:c0 + n * W]).then_inc(T.sem.st, 16)
+        stores += 1
+    g.wait_ge(T.sem.st, 16 * stores)
+    g.wait_ge(T.sem.snd, sent)

@@ -10,19 +10,25 @@ SCRATCH = {
     "g1": ("dram", [8, 128, 2], "float32"),
     "r1": ("dram", [128, 2], "float32"),
 }
-SEMAPHORES = ["ld1", "ld2", "st", "snd", "hx", "a01", "a23", "a45", "a67", "g", "r"]
+SEMAPHORES = ["ld1", "ld2", "st", "snd", "g", "r", "hx", "a01", "a23", "a45", "a67"]
 
-CALLS = {
+SCRIPT = {
     2: [
-        [(0xFF00, ["h6"], "hx"), (0x000F, [2], "a23"), (0x00F0, [1], "a01")],
-        [(0x000F, [4], "a45"), (0x00F0, [3], "a23")],
-        [(0x00FF, [6], "a67")],
+        ("call", [(0xFF00, 0, ["h6"], "hx"), (0x000F, 0, [2], "a23"), (0x00F0, 0, [1], "a01")]),
+        ("x1",),
+        ("call", [(0x000F, 0, [4], "a45"), (0x00F0, 0, [3], "a23")]),
+        ("call", [(0x00FF, 0, [6], "a67")]),
+        ("wait", "a01"), ("store", 0, 2),
+        ("wait", "a23"), ("store", 2, 2),
+        ("y1",),
+        ("wait", "a45"), ("store", 4, 2),
+        ("wait", "a67"), ("store", 6, 2),
     ],
     6: [
-        [(0x000F, [5], "a45"), (0x00F0, [7], "a67")],
+        ("wait", "hx"),
+        ("call", [(0x000F, 0, [5], "a45"), (0x00F0, 0, [7], "a67")]),
     ],
 }
-STORES = [("a01", 0, 2), ("a23", 2, 2), "y1", ("a45", 4, 2), ("a67", 6, 2)]
 
 
 def bits(mask):
@@ -31,11 +37,12 @@ def bits(mask):
 
 def arrivals(sem):
     n = 0
-    for calls in CALLS.values():
-        for call in calls:
-            for mask, dsts, s in call:
-                if s == sem:
-                    n += bits(mask) * len(dsts)
+    for script in SCRIPT.values():
+        for step in script:
+            if step[0] == "call":
+                for mask, blk, dsts, s in step[1]:
+                    if s == sem:
+                        n += bits(mask) * len(dsts)
     return n
 
 
@@ -49,28 +56,10 @@ def rank_program(g, core, T, topo):
         a = topo.addr(c)
         return bass.DstId(rid=a[0], pnc=a[1])
 
-    def sem(name):
-        return {"hx": T.sem.hx, "a01": T.sem.a01, "a23": T.sem.a23, "a45": T.sem.a45, "a67": T.sem.a67}[name]
+    sems = {"hx": T.sem.hx, "a01": T.sem.a01, "a23": T.sem.a23, "a45": T.sem.a45, "a67": T.sem.a67}
 
-    own = T.land[:, W * r:W * (r + 1)]
-    sent = 0
-
-    def send_block():
-        n = 0
-        for call in CALLS[k]:
-            trs = []
-            for mask, dsts, s in call:
-                ids = []
-                for d in dsts:
-                    if isinstance(d, str):
-                        ids.append(did(8 * chip + int(d[1:])))
-                    else:
-                        ids.append(did(T.cores[r ^ d]))
-                trs.append(bass.RemoteDMATransfer(dst_ids=ids, dma_engine_mask=mask, remote_sem=sem(s),
-                                                  srcs=[own], dsts=[own] * len(ids), alu_op=0))
-                n += bits(mask)
-            g.remote_dma_fused(trs, local_sem=T.sem.snd)
-        return n
+    def block(j):
+        return T.land[:, W * j:W * (j + 1)]
 
     if k == FOLD_K:
         g.wait_ge(T.sem.g, 8)
@@ -79,33 +68,49 @@ def rank_program(g, core, T, topo):
                                                    dsts=[T.r1[:]], alu_op=1)], local_sem=T.sem.snd)
         g.wait_ge(T.sem.snd, 1)
         return
-
-    if k != RANK_K:
-        if k in CALLS:
-            g.wait_ge(T.sem.hx, arrivals("hx"))
-            sent = send_block()
-            g.wait_ge(T.sem.snd, sent)
+    if k not in SCRIPT:
         return
 
-    g.dma_start(T.s1[:], T.x1[:]).then_inc(T.sem.ld1, 16)
-    g.dma_start(own, T.x2[:]).then_inc(T.sem.ld2, 16)
-    g.wait_ge(T.sem.ld1, 16)
-    g.remote_dma_fused([bass.RemoteDMATransfer(dst_ids=[did(T.cores[j] - RANK_K + FOLD_K)], dma_engine_mask=1 << j,
-                                               remote_sem=T.sem.g, srcs=[T.s1[:]], dsts=[T.g1[r]], alu_op=0)
-                        for j in range(8)], local_sem=T.sem.snd)
-    sent += 8
-    g.wait_ge(T.sem.ld2, 16)
-    sent += send_block()
+    sent = 0
     stores = 0
-    for s in STORES:
-        if s == "y1":
+    if k == RANK_K:
+        g.dma_start(block(r), T.x2[:]).then_inc(T.sem.ld2, 16)
+        g.dma_start(T.s1[:], T.x1[:]).then_inc(T.sem.ld1, 16)
+        g.wait_ge(T.sem.ld2, 16)
+
+    for step in SCRIPT[k]:
+        if step[0] == "call":
+            trs = []
+            for mask, blk, dsts, s in step[1]:
+                ids = []
+                for d in dsts:
+                    if isinstance(d, str):
+                        ids.append(did(8 * chip + int(d[1:])))
+                    else:
+                        ids.append(did(T.cores[r ^ d]))
+                ap = block(r ^ blk)
+                trs.append(bass.RemoteDMATransfer(dst_ids=ids, dma_engine_mask=mask, remote_sem=sems[s],
+                                                  srcs=[ap], dsts=[ap] * len(ids), alu_op=0))
+                sent += bits(mask)
+            g.remote_dma_fused(trs, local_sem=T.sem.snd)
+        elif step[0] == "x1":
+            g.wait_ge(T.sem.ld1, 16)
+            g.remote_dma_fused([bass.RemoteDMATransfer(dst_ids=[did(T.cores[j] - RANK_K + FOLD_K)],
+                                                       dma_engine_mask=1 << j, remote_sem=T.sem.g,
+                                                       srcs=[T.s1[:]], dsts=[T.g1[r]], alu_op=0)
+                                for j in range(8)], local_sem=T.sem.snd)
+            sent += 8
+        elif step[0] == "wait":
+            g.wait_ge(sems[step[1]], arrivals(step[1]))
+        elif step[0] == "store":
+            n = step[2]
+            c0 = ((r ^ step[1]) // n) * n * W
+            g.dma_start(T.y2[:, c0:c0 + n * W], T.land[:, c0:c0 + n * W]).then_inc(T.sem.st, 16)
+            stores += 1
+        else:
             g.wait_ge(T.sem.r, 1)
             g.dma_start(T.y1[:], T.r1[:]).then_inc(T.sem.st, 16)
-        else:
-            name, d0, n = s
-            g.wait_ge(sem(name), arrivals(name))
-            c0 = ((r ^ d0) // n) * n * W
-            g.dma_start(T.y2[:, c0:c0 + n * W], T.land[:, c0:c0 + n * W]).then_inc(T.sem.st, 16)
-        stores += 1
-    g.wait_ge(T.sem.st, 16 * stores)
+            stores += 1
+    if stores:
+        g.wait_ge(T.sem.st, 16 * stores)
     g.wait_ge(T.sem.snd, sent)

@@ -10,23 +10,22 @@ SCRATCH = {
     "g1": ("dram", [8, 128, 2], "float32"),
     "r1": ("dram", [128, 2], "float32"),
 }
-SEMAPHORES = ["ld1", "ld2", "st", "snd", "g", "r", "hx", "a01", "a23", "a45", "a67"]
+SEMAPHORES = ["ld1", "ld2", "st", "snd", "g", "r", "hx", "a01", "a23", "a47"]
 
 SCRIPT = {
     2: [
         ("call", [(0xFF00, 0, ["h6"], "hx"), (0x000F, 0, [2], "a23"), (0x00F0, 0, [1], "a01")]),
         ("x1",),
-        ("call", [(0x000F, 0, [4], "a45"), (0x00F0, 0, [3], "a23")]),
-        ("call", [(0x00FF, 0, [6], "a67")]),
+        ("call", [(0x000F, 0, [4], "a47"), (0x00F0, 0, [3], "a23")]),
+        ("call", [(0x00FF, 0, [6], "a47")]),
         ("wait", "a01"), ("store", 0, 2),
         ("wait", "a23"), ("store", 2, 2),
         ("y1",),
-        ("wait", "a45"), ("store", 4, 2),
-        ("wait", "a67"), ("store", 6, 2),
+        ("wait", "a47"), ("store", 4, 4),
     ],
     6: [
-        ("wait", "hx"),
-        ("call", [(0x000F, 0, [5], "a45"), (0x00F0, 0, [7], "a67")]),
+        ("wait", "hx", 8),
+        ("call", [(0x000F, 0, [5], "a47"), (0x00F0, 0, [7], "a47")]),
     ],
 }
 
@@ -56,7 +55,7 @@ def rank_program(g, core, T, topo):
         a = topo.addr(c)
         return bass.DstId(rid=a[0], pnc=a[1])
 
-    sems = {"hx": T.sem.hx, "a01": T.sem.a01, "a23": T.sem.a23, "a45": T.sem.a45, "a67": T.sem.a67}
+    sems = {"hx": T.sem.hx, "a01": T.sem.a01, "a23": T.sem.a23, "a47": T.sem.a47}
 
     def block(j):
         return T.land[:, W * j:W * (j + 1)]
@@ -101,7 +100,7 @@ def rank_program(g, core, T, topo):
                                 for j in range(8)], local_sem=T.sem.snd)
             sent += 8
         elif step[0] == "wait":
-            g.wait_ge(sems[step[1]], arrivals(step[1]))
+            g.wait_ge(sems[step[1]], step[2] if len(step) > 2 else arrivals(step[1]))
         elif step[0] == "store":
             n = step[2]
             c0 = ((r ^ step[1]) // n) * n * W

@@ -20,8 +20,8 @@ SCRIPT = {
         ("call", [(0x00FF, 0, [6], "a47")]),
         ("wait", "a01"), ("store", 0, 2),
         ("wait", "a23"), ("store", 2, 2),
-        ("y1",),
         ("wait", "a47"), ("store", 4, 4),
+        ("y1",),
     ],
     6: [
         ("wait", "hx", 8),

import concourse.bass as bass

RANK_K = 2
FOLD_K = 1
W = 512

SCRATCH = {
    "land": ("sbuf", [128, 4096], "bfloat16"),
    "s1": ("dram", [128, 2], "float32"),
    "g1": ("dram", [8, 128, 2], "float32"),
    "r1": ("dram", [128, 2], "float32"),
}
SEMAPHORES = ["ld1", "ld2", "st", "snd", "g", "r", "hx", "a01", "a23", "a47"]

SCRIPT = {
    2: [
        ("call", [(0xFF00, 0, ["h6"], "hx"), (0x000F, 0, [2], "a23"), (0x00F0, 0, [1], "a01")]),
        ("x1",),
        ("call", [(0x000F, 0, [4], "a47"), (0x00F0, 0, [3], "a23")]),
        ("call", [(0x00FF, 0, [6], "a47")]),
        ("wait", "a01"), ("store", 0, 2),
        ("wait", "a23"), ("store", 2, 2),
        ("wait", "a47"), ("store", 4, 4),
        ("y1",),
    ],
    6: [
        ("wait", "hx", 8),
        ("call", [(0x000F, 0, [5], "a47"), (0x00F0, 0, [7], "a47")]),
    ],
}


def bits(mask):
    return bin(mask).count("1")


def arrivals(sem):
    n = 0
    for script in SCRIPT.values():
        for step in script:
            if step[0] == "call":
                for mask, blk, dsts, s in step[1]:
                    if s == sem:
                        n += bits(mask) * len(dsts)
    return n


def rank_program(g, core, T, topo):
    chip, k = topo.chip(core), core % 8
    r = T.rank_of(8 * chip + RANK_K)
    if r is None:
        return

    def did(c):
        a = topo.addr(c)
        return bass.DstId(rid=a[0], pnc=a[1])

    sems = {"hx": T.sem.hx, "a01": T.sem.a01, "a23": T.sem.a23, "a47": T.sem.a47}

    def block(j):
        return T.land[:, W * j:W * (j + 1)]

    if k == FOLD_K:
        g.wait_ge(T.sem.g, 8)
        g.remote_dma_fused([bass.RemoteDMATransfer(dst_ids=[did(8 * chip + RANK_K)], dma_engine_mask=1,
                                                   remote_sem=T.sem.r, srcs=[T.g1[j] for j in range(8)],
                                                   dsts=[T.r1[:]], alu_op=1)], local_sem=T.sem.snd)
        g.wait_ge(T.sem.snd, 1)
        return
    if k not in SCRIPT:
        return

    sent = 0
    stores = 0
    if k == RANK_K:
        g.dma_start(block(r), T.x2[:]).then_inc(T.sem.ld2, 16)
        g.dma_start(T.s1[:], T.x1[:]).then_inc(T.sem.ld1, 16)
        g.wait_ge(T.sem.ld2, 16)

    for step in SCRIPT[k]:
        if step[0] == "call":
            trs = []
            for mask, blk, dsts, s in step[1]:
                ids = []
                for d in dsts:
                    if isinstance(d, str):
                        ids.append(did(8 * chip + int(d[1:])))
                    else:
                        ids.append(did(T.cores[r ^ d]))
                ap = block(r ^ blk)
                trs.append(bass.RemoteDMATransfer(dst_ids=ids, dma_engine_mask=mask, remote_sem=sems[s],
                                                  srcs=[ap], dsts=[ap] * len(ids), alu_op=0))
                sent += bits(mask)
            g.remote_dma_fused(trs, local_sem=T.sem.snd)
        elif step[0] == "x1":
            g.wait_ge(T.sem.ld1, 16)
            g.remote_dma_fused([bass.RemoteDMATransfer(dst_ids=[did(T.cores[j] - RANK_K + FOLD_K)],
                                                       dma_engine_mask=1 << j, remote_sem=T.sem.g,
                                                       srcs=[T.s1[:]], dsts=[T.g1[r]], alu_op=0)
                                for j in range(8)], local_sem=T.sem.snd)
            sent += 8
        elif step[0] == "wait":
            g.wait_ge(sems[step[1]], step[2] if len(step) > 2 else arrivals(step[1]))
        elif step[0] == "store":
            n = step[2]
            c0 = ((r ^ step[1]) // n) * n * W
            g.dma_start(T.y2[:, c0:c0 + n * W], T.land[:, c0:c0 + n * W]).then_inc(T.sem.st, 16)
            stores += 1
        else:
            g.wait_ge(T.sem.r, 1)
            g.dma_start(T.y1[:], T.r1[:]).then_inc(T.sem.st, 16)
            stores += 1
    if stores:
        g.wait_ge(T.sem.st, 16 * stores)
    g.wait_ge(T.sem.snd, sent)
